import numpy as np
import ml_dtypes


def mxq(x, axis, fmt="e4m3"):
    dtype, down = {"e4m3": (ml_dtypes.float8_e4m3fn, 7), "e5m2": (ml_dtypes.float8_e5m2, 14)}[fmt]
    v = np.moveaxis(np.asarray(x, np.float32).astype(ml_dtypes.bfloat16).astype(np.float64), axis, -1)
    blocks = v.reshape(v.shape[:-1] + (-1, 32))
    amax = np.abs(blocks).max(-1, keepdims=True)
    byte = np.maximum(np.where(amax > 0, np.frexp(amax)[1] - 1 + 127, 0) - down, 1)
    scale = np.exp2(byte - 127.0)
    codes = (blocks / scale).astype(np.float32).astype(dtype).astype(np.float64)
    return np.moveaxis((codes * scale).reshape(v.shape), -1, axis)


WIDE = False


def mx_kscale(k):
    if not WIDE:
        return np.ones(k)
    levels = np.array([10, -10, 5, -5, 0])
    if k % 512:
        return np.exp2(np.random.permutation(np.resize(levels, k // 32))).repeat(32)
    a = np.empty((k // 512, 16))
    for p in range(k // 512):
        a[p, :8] = np.random.permutation(np.resize(levels, 8))
        for g in range(8):
            far = levels[np.abs(levels - a[p, g]) >= 10]
            a[p, g + 8] = far[np.random.randint(len(far))]
    return np.exp2(a.ravel()).repeat(32)


def f64(x):
    return np.asarray(x).astype(np.float64)


def striped(idx):
    return np.tile(idx.reshape(-1, 16).T, (8, 1)).astype(np.uint16)


def unstriped(offs):
    return offs[:16].T.reshape(-1).astype(np.int64)


E2M1 = np.array([0.0, 0.5, 1.0, 1.5, 2.0, 3.0, 4.0, 6.0, -0.0, -0.5, -1.0, -1.5, -2.0, -3.0, -4.0, -6.0])


def pack_weight(w, fmt):
    k, n = w.shape
    w = f64(np.asarray(w, np.float32).astype(ml_dtypes.bfloat16)).reshape(k // 32, 32, n)
    amax = np.abs(w).max(1)
    if fmt == "e4m3":
        byte = np.frexp(amax)[1] - 1 + 127 - 7
    else:
        mant, ex = np.frexp(amax / 6.0)
        byte = np.where(mant > 0.5, ex, ex - 1) + 127
    byte = np.clip(np.where(amax > 0, byte, 1), 1, 254)
    scaled = (w * np.exp2(127.0 - byte)[:, None, :]).reshape(k, n).astype(np.float32)
    by_word = np.ascontiguousarray(scaled.reshape(k // 512, 128, 4, n).transpose(0, 1, 3, 2))
    if fmt == "e4m3":
        words = by_word.astype(ml_dtypes.float8_e4m3fn).view(np.uint8)
    else:
        c = by_word.astype(ml_dtypes.float4_e2m1fn).view(np.uint8) & 0xF
        words = (c[..., 0::2] | (c[..., 1::2] << 4)).reshape(k // 512, 128, 2 * n)
    return np.ascontiguousarray(words), np.ascontiguousarray(byte.astype(np.uint8).reshape(k // 512, 16, n))


def unpack_weight(words, scales, fmt):
    g, _, n = scales.shape
    words = np.ascontiguousarray(words).reshape(g, 128, n, -1)
    if fmt == "e4m3":
        vals = words.view(ml_dtypes.float8_e4m3fn).astype(np.float64)
    else:
        nib = np.empty((g, 128, n, 4), np.uint8)
        nib[..., 0::2] = words & 0xF
        nib[..., 1::2] = words >> 4
        vals = E2M1[nib]
    vals = vals * np.repeat(np.exp2(scales.astype(np.float64) - 127.0), 8, axis=1)[..., None]
    return vals.transpose(0, 1, 3, 2).reshape(g * 512, n)


def gelu(v):
    return 0.5 * v * (1.0 + np.tanh(np.sqrt(2.0 / np.pi) * (v + 0.044715 * v**3)))


def bf(x):
    return np.asarray(x, np.float32).astype(ml_dtypes.bfloat16)


def planes(Y):
    n, m = Y.shape
    b = f64(bf(Y)).reshape(n // 32, 32, m)
    amax = np.abs(b).max(1)
    byte = np.clip(np.where(amax > 0, np.frexp(amax)[1] - 1 + 127 - 7, 1), 1, 254)
    codes = (b * np.exp2(127.0 - byte)[:, None, :]).reshape(n, m).astype(np.float32).astype(ml_dtypes.float8_e4m3fn).view(np.uint8)
    words = codes.reshape(n // 512, 128, 4, m).transpose(0, 1, 3, 2)
    return np.ascontiguousarray(words), np.ascontiguousarray(byte.astype(np.uint8).reshape(n // 512, 16, m))


K, T, S, H, N, P = 1024, 4096, 1024, 1024, 512, 512

def setup_inputs():
    n = np.random.standard_normal
    s = mx_kscale(K)[:, None]
    u = mx_kscale(H)[:, None]
    d = {}
    d["tab_words"], d["tab_scales"] = pack_weight(n((K, T)) * s, "e4m3")
    d["offs"] = striped(np.random.permutation(T)[:S])
    d["pos1"] = striped(np.random.permutation(S)[:P])
    d["pos2"] = striped(np.random.permutation(S)[:P])
    d["w1"] = (n((K, H)) / K**0.5 / s).astype(np.float32)
    d["sens"] = (1.3 * np.exp(0.3 * n(H))).astype(np.float32)
    d["room"] = (0.9 * n((H, S))).astype(np.float32)
    d["gain"] = (1.2 * np.exp(0.3 * n(H)) * u[:, 0]).astype(np.float32)
    size = np.exp(0.8 * n(N))[None, :]
    d["w4_words"], d["w4_scales"] = pack_weight(n((H, N)) / H**0.5 * size / u, "e2m1")
    d["w3"] = (n((H, N)) / H**0.5 * size / u).astype(np.float32)
    return d

def reference(tab_words, tab_scales, offs, pos1, pos2, w1, sens, room, gain, w4_words, w4_scales, w3):
    v = unpack_weight(tab_words, tab_scales, "e4m3")[:, unstriped(offs)]
    w4 = unpack_weight(w4_words, w4_scales, "e2m1")
    b = mxq(f64(w1), 0, "e4m3").T @ v
    x = f64(sens)[:, None] * b + f64(room)
    h = x / (1.0 + np.exp(-x)) * f64(gain)[:, None]
    hq = mxq(h, 0, "e4m3")
    low = w4.T @ hq
    dev = mxq(f64(w3), 0, "e4m3").T @ hq
    e = np.maximum(low, np.abs(dev))
    y = e[:, unstriped(pos1)] + e[:, unstriped(pos2)]
    words, scales = planes(y)
    return y, words, scales

@@ -1,0 +1,257 @@
+from contextlib import ExitStack
+
+import concourse.mybir as mybir
+
+K, T, S, H, N, M = 1024, 4096, 1024, 1024, 512, 512
+FLOPS = 2 * K * H * S + 2 * 2 * H * N * S
+
+F32 = mybir.dt.float32
+BF16 = mybir.dt.bfloat16
+I32 = mybir.dt.int32
+U32 = mybir.dt.uint32
+U16 = mybir.dt.uint16
+U8 = mybir.dt.uint8
+FP8X4 = mybir.dt.float8_e4m3fn_x4
+FP4X4 = mybir.dt.float4_e2m1fn_x4
+ALU = mybir.AluOpType
+ACT = mybir.ActivationFunctionType
+
+P = 128
+BANK = 512
+
+
+def tile_list_crate_pair_features_kernel(
+    tc, tab_words, tab_scales, offs, pos1, pos2, w1, sens, room, gain, w4_words, w4_scales, w3,
+    out_0, out_1, out_2,
+):
+    nc = tc.nc
+    with ExitStack() as ctx:
+        keep = ctx.enter_context(tc.tile_pool(name="keep", bufs=1))
+        ring = ctx.enter_context(tc.tile_pool(name="ring", bufs=2))
+        psum = ctx.enter_context(tc.psum_pool(name="psum", bufs=1))
+
+        tab_scale_rows = keep.tile([P, T], U8)
+        w4_scale_rows = keep.tile([P, 2, N], U8)
+        nc.vector.memset(tab_scale_rows[:].bitcast(I32), 0)
+        nc.vector.memset(w4_scale_rows[:].rearrange("p g n -> p (g n)").bitcast(I32), 0)
+        for q in range(4):
+            nc.gpsimd.dma_start(
+                out=tab_scale_rows[32 * q : 32 * q + 8, :].bitcast(I32),
+                in_=tab_scales[:, 4 * q : 4 * q + 4, :].bitcast(I32),
+            )
+        for q in range(4):
+            nc.gpsimd.dma_start(
+                out=w4_scale_rows[32 * q : 32 * q + 4, :, :].bitcast(I32),
+                in_=w4_scales[:, 4 * q : 4 * q + 4, :].rearrange("g r n -> r g n").bitcast(I32),
+            )
+
+        warm = keep.tile([P, 8], F32)
+        warm_out = keep.tile([P, 8], F32)
+        nc.vector.memset(warm[:], 0.0)
+        nc.scalar.activation(warm_out[:], warm[:], ACT.Silu)
+
+        def load_weight(w, row0, col0):
+            raw = ring.tile([P, 4, BANK], F32, name="w_raw", bufs=4)
+            nc.sync.dma_start(
+                out=raw[:], in_=w[row0 : row0 + 512, col0 : col0 + BANK].rearrange("(p j) c -> p j c", j=4)
+            )
+            return raw
+
+        def load_room(g, half, t0, nt):
+            raw = keep.tile([P, nt, BANK], F32, name="room_%d_%d_%d" % (g, half, t0))
+            rows = room[512 * g : 512 * g + 512, BANK * half : BANK * half + BANK].rearrange("(p t) j -> p t j", t=4)
+            nc.sync.dma_start(out=raw[:], in_=rows[:, t0 : t0 + nt, :])
+            return [raw[:, t, :] for t in range(nt)]
+
+        def load_table(a):
+            words = keep.tile([P, T], I32, name="tab_%d" % a)
+            nc.sync.dma_start(out=words[:], in_=tab_words[a].rearrange("p n t -> p (n t)").bitcast(I32))
+            return words
+
+        w1_raw = {}
+        w1_raw[0, 0] = load_weight(w1, 0, 0)
+        w1_raw[0, 1] = load_weight(w1, 512, 0)
+        idx = keep.tile([P, S // 16], U16)
+        nc.sync.dma_start(idx[:], offs)
+        w4_raw = keep.tile([P, 2, 2 * N], U8)
+        nc.sync.dma_start(out=w4_raw[:].bitcast(I32), in_=w4_words.rearrange("g p n -> p g n").bitcast(I32))
+        sens_sb = keep.tile([P, 2, 4], F32)
+        gain_sb = keep.tile([P, 2, 4], F32)
+        nc.sync.dma_start(out=sens_sb[:], in_=sens.rearrange("(g p t) -> p g t", g=2, t=4))
+        nc.sync.dma_start(out=gain_sb[:], in_=gain.rearrange("(g p t) -> p g t", g=2, t=4))
+        tab = [load_table(0)]
+        p1 = keep.tile([P, M // 16], U16)
+        p2 = keep.tile([P, M // 16], U16)
+        nc.sync.dma_start(p1[:], pos1)
+        nc.sync.dma_start(p2[:], pos2)
+        tab.append(load_table(1))
+        room_sb = {}
+        room_sb[0, 0] = [load_room(0, 0, t, 1)[0] for t in range(4)]
+        room_sb[0, 1] = load_room(0, 1, 0, 4)
+        w1_raw[1, 0] = load_weight(w1, 0, 512)
+        w1_raw[1, 1] = load_weight(w1, 512, 512)
+        w3_raw = [load_weight(w3, 0, 0)]
+        room_sb[1, 0] = load_room(1, 0, 0, 4)
+        room_sb[1, 1] = load_room(1, 1, 0, 4)
+        w3_raw.append(load_weight(w3, 512, 0))
+
+        def round_weight(raw):
+            grouped = ring.tile([P, 4, P, 4], BF16, name="w_grouped", align_bytes=64)
+            src = raw[:].rearrange("p j (q t) -> p q j t", t=4)
+            dst = grouped[:].rearrange("p t q j -> p q j t")
+            for t0 in (0, 2):
+                nc.scalar.copy(out=dst[:, :, :, t0 : t0 + 2], in_=src[:, :, :, t0 : t0 + 2])
+            return grouped
+
+        def quantize(grouped_2d, width, name):
+            codes = keep.tile([P, width], I32, name=name + "_codes", align_bytes=64)
+            scales = keep.tile([P, width], U8, name=name + "_scales", align_bytes=64)
+            nc.vector.quantize_mx(out=codes[:].bitcast(FP8X4), scales=scales[:], in_=grouped_2d)
+            return codes, scales
+
+        def quantize_weight(grouped, name):
+            return quantize(grouped[:].rearrange("p t q j -> p (t q j)"), BANK, name)
+
+        w4_codes = keep.tile([P, 2, 4, P, 2], U8, align_bytes=64)
+        w4_sc = keep.tile([P, 2, 4, P], U8, align_bytes=64)
+        for g in range(2):
+            nc.vector.tensor_copy(
+                out=w4_codes[:, g].rearrange("p t q b -> p q t b"),
+                in_=w4_raw[:, g, :].rearrange("p (q t b) -> p q t b", t=4, b=2),
+            )
+        gain_pairs = keep.tile([P, 2, 4, 2], F32)
+        for i in range(2):
+            nc.vector.tensor_copy(out=gain_pairs[:, :, :, i], in_=gain_sb[:])
+
+        v_scales = keep.tile([P, S], U8, align_bytes=64)
+        nc.vector.tensor_copy(v_scales[:], tab_scale_rows[:].indirect(idx[:]))
+
+        w1_q = {}
+        for a in range(2):
+            w1_q[0, a] = quantize_weight(round_weight(w1_raw[0, a]), "w1_0_%d" % a)
+        v_codes = {}
+        for a in range(2):
+            for half in range(2):
+                picked = keep.tile([P, BANK], U32, name="v_%d_%d" % (a, half), align_bytes=64)
+                nc.vector.tensor_copy(
+                    picked[:], tab[a][:].bitcast(U32).indirect(idx[:, 32 * half : 32 * half + 32])
+                )
+                v_codes[a, half] = picked
+
+        nc.vector.tensor_copy(
+            out=w4_sc[:].rearrange("p g t q -> p g q t"),
+            in_=w4_scale_rows[:].rearrange("p g (q t) -> p g q t", t=4),
+        )
+
+        def first_stage(g, half):
+            act = ring.tile([P, 4, BANK], F32, name="act")
+            for t in range(4):
+                acc = psum.tile([P, BANK], F32, name="bank_%d" % (4 * half + t))
+                for a in range(2):
+                    codes, scales = w1_q[g, a]
+                    nc.tensor.matmul_mx(
+                        out=acc[:],
+                        lhsT=codes[:, P * t : P * t + P].bitcast(FP8X4),
+                        lhsT_scale=scales[:, P * t : P * t + P],
+                        rhs=v_codes[a, half][:].bitcast(FP8X4),
+                        rhs_scale=v_scales[4 * a : P, BANK * half : BANK * half + BANK],
+                        start=(a == 0),
+                        stop=(a == 1),
+                    )
+                x = ring.tile([P, BANK], F32, name="x", bufs=4)
+                nc.vector.scalar_tensor_tensor(
+                    out=x[:], in0=acc[:], scalar=sens_sb[:, g, t : t + 1], in1=room_sb[g, half][t],
+                    op0=ALU.mult, op1=ALU.add,
+                )
+                nc.scalar.activation(act[:, t, :], x[:], ACT.Silu)
+            return act
+
+        def make_h(act, g, half):
+            grouped = ring.tile([P, BANK, 4], BF16, name="h_grouped", align_bytes=64)
+            nc.vector.tensor_tensor(
+                out=grouped[:].rearrange("p (c i) t -> p c t i", i=2),
+                in0=act[:].rearrange("p t (c i) -> p c t i", i=2),
+                in1=gain_pairs[:, g : g + 1, :, :].to_broadcast([P, BANK // 2, 4, 2]),
+                op=ALU.mult,
+            )
+            return quantize(grouped[:].rearrange("p j t -> p (j t)"), BANK, "h_%d_%d" % (g, half))
+
+        h_q = {}
+        act00 = first_stage(0, 0)
+        act01 = first_stage(0, 1)
+        h_q[0, 0] = make_h(act00, 0, 0)
+        w1_q[1, 0] = quantize_weight(round_weight(w1_raw[1, 0]), "w1_1_0")
+        w1_q[1, 1] = quantize_weight(round_weight(w1_raw[1, 1]), "w1_1_1")
+        h_q[0, 1] = make_h(act01, 0, 1)
+        w3_grouped = round_weight(w3_raw[0])
+        act10 = first_stage(1, 0)
+        w3_q = [quantize_weight(w3_grouped, "w3_0")]
+        act11 = first_stage(1, 1)
+        w3_grouped = round_weight(w3_raw[1])
+        h_q[1, 0] = make_h(act10, 1, 0)
+        w3_q.append(quantize_weight(w3_grouped, "w3_1"))
+        h_q[1, 1] = make_h(act11, 1, 1)
+
+        e = [keep.tile([P, S], F32, name="e_%d" % t) for t in range(4)]
+        for half in range(2):
+            for t in range(4):
+                dev = psum.tile([P, BANK], F32, name="bank_%d" % (2 * t))
+                low = psum.tile([P, BANK], F32, name="bank_%d" % (2 * t + 1))
+                for g in range(2):
+                    codes, scales = h_q[g, half]
+                    nc.tensor.matmul_mx(
+                        out=dev[:],
+                        lhsT=w3_q[g][0][:, P * t : P * t + P].bitcast(FP8X4),
+                        lhsT_scale=w3_q[g][1][:, P * t : P * t + P],
+                        rhs=codes[:].bitcast(FP8X4), rhs_scale=scales[:],
+                        start=(g == 0), stop=(g == 1),
+                    )
+                for g in range(2):
+                    codes, scales = h_q[g, half]
+                    nc.tensor.matmul_mx(
+                        out=low[:],
+                        lhsT=w4_codes[:, g, t].rearrange("p q b -> p (q b)").bitcast(FP4X4),
+                        lhsT_scale=w4_sc[:, g, t, :],
+                        rhs=codes[:].bitcast(FP8X4), rhs_scale=scales[:],
+                        start=(g == 0), stop=(g == 1),
+                    )
+                size = ring.tile([P, BANK], F32, name="size", bufs=4)
+                nc.scalar.activation(size[:], dev[:], ACT.Abs)
+                nc.vector.tensor_tensor(
+                    out=e[t][:, BANK * half : BANK * half + BANK], in0=low[:], in1=size[:], op=ALU.max
+                )
+
+        y_codes = keep.tile([P, M], I32, align_bytes=64)
+        y_scales = keep.tile([P, M], U8, align_bytes=64)
+        y_grouped = keep.tile([P, M, 4], BF16, align_bytes=64)
+        out_rows = out_0.rearrange("(p t) m -> p t m", t=4)
+        out_words = out_1[0].rearrange("p m t -> p (m t)").bitcast(I32)
+
+        def pair_up(t, m0, width):
+            places = slice(m0 // 16, (m0 + width) // 16)
+            upper = ring.tile([P, width], F32, name="upper")
+            y = keep.tile([P, width], F32, name="y_%d_%d" % (t, m0))
+            nc.vector.tensor_copy(upper[:], e[t][:].indirect(p1[:, places]))
+            nc.vector.tensor_tensor(y[:], e[t][:].indirect(p2[:, places]), upper[:], ALU.add)
+            nc.scalar.copy(out=y_grouped[:, m0 : m0 + width, t], in_=y[:])
+            nc.sync.dma_start(out=out_rows[:, t, m0 : m0 + width], in_=y[:])
+
+        def planes(m0, width):
+            nc.vector.quantize_mx(
+                out=y_codes[:, m0 : m0 + width].bitcast(FP8X4),
+                scales=y_scales[:, m0 : m0 + width],
+                in_=y_grouped[:, m0 : m0 + width, :].rearrange("p m t -> p (m t)"),
+            )
+            nc.sync.dma_start(out=out_words[:, m0 : m0 + width], in_=y_codes[:, m0 : m0 + width])
+
+        for t in range(3):
+            pair_up(t, 0, M)
+        pair_up(3, 0, 256)
+        pair_up(3, 256, 256)
+        planes(0, 256)
+        planes(256, 256)
+        for q, queue in enumerate((nc.scalar, nc.sync, nc.scalar, nc.sync)):
+            queue.dma_start(
+                out=out_2[0, 4 * q : 4 * q + 4, :].bitcast(I32),
+                in_=y_scales[32 * q : 32 * q + 4, :].bitcast(I32),
+            )

@@ -18,6 +18,13 @@ ACT = mybir.ActivationFunctionType
 
 P = 128
 BANK = 512
+HB = 1
+WB = 3
+V = [(512,"V","")]
+LOADS = [("r",0,1),("w1",0),("w1",1),("r",1,0),("r",1,1),("w3",0),("w3",1)]
+STEPS = [("A",0,0),("A",0,1),("w1",0,0,"S"),("w1",1,0,"S"),("w1",0,2,"S"),("w1",1,2,"S"),("C",0,0,V),("C",0,1,[(256,"V",""),(256,"S","S")]),("A",1,0),("A",1,1),("w3",0,0,"S"),("w3",1,0,"S"),("C",1,0,V),("C",1,1,V),
+ ("E",0,0,0),("E",1,0,2),("E",0,1,4),("E",1,1,6),("w3",0,2,"S"),("w3",1,2,"S"),("Y",0,0,512),("E",2,0,0),("E",2,1,2),("Y",1,0,512),("E",3,0,4),("E",3,1,6),("Y",2,0,512),
+ ("Y",3,0,256),("Y",3,256,256),("P",0,256),("P",256,256)]
 
 
 def tile_list_crate_pair_features_kernel(
@@ -34,16 +41,6 @@ def tile_list_crate_pair_features_kernel(
         w4_scale_rows = keep.tile([P, 2, N], U8)
         nc.vector.memset(tab_scale_rows[:].bitcast(I32), 0)
         nc.vector.memset(w4_scale_rows[:].rearrange("p g n -> p (g n)").bitcast(I32), 0)
-        for q in range(4):
-            nc.gpsimd.dma_start(
-                out=tab_scale_rows[32 * q : 32 * q + 8, :].bitcast(I32),
-                in_=tab_scales[:, 4 * q : 4 * q + 4, :].bitcast(I32),
-            )
-        for q in range(4):
-            nc.gpsimd.dma_start(
-                out=w4_scale_rows[32 * q : 32 * q + 4, :, :].bitcast(I32),
-                in_=w4_scales[:, 4 * q : 4 * q + 4, :].rearrange("g r n -> r g n").bitcast(I32),
-            )
 
         warm = keep.tile([P, 8], F32)
         warm_out = keep.tile([P, 8], F32)
@@ -70,7 +67,6 @@ def tile_list_crate_pair_features_kernel(
 
         w1_raw = {}
         w1_raw[0, 0] = load_weight(w1, 0, 0)
-        w1_raw[0, 1] = load_weight(w1, 512, 0)
         idx = keep.tile([P, S // 16], U16)
         nc.sync.dma_start(idx[:], offs)
         w4_raw = keep.tile([P, 2, 2 * N], U8)
@@ -79,28 +75,42 @@ def tile_list_crate_pair_features_kernel(
         gain_sb = keep.tile([P, 2, 4], F32)
         nc.sync.dma_start(out=sens_sb[:], in_=sens.rearrange("(g p t) -> p g t", g=2, t=4))
         nc.sync.dma_start(out=gain_sb[:], in_=gain.rearrange("(g p t) -> p g t", g=2, t=4))
-        tab = [load_table(0)]
         p1 = keep.tile([P, M // 16], U16)
         p2 = keep.tile([P, M // 16], U16)
         nc.sync.dma_start(p1[:], pos1)
         nc.sync.dma_start(p2[:], pos2)
+        w1_raw[0, 1] = load_weight(w1, 512, 0)
+        for q in range(4):
+            nc.sync.dma_start(
+                out=tab_scale_rows[32 * q : 32 * q + 8, :].bitcast(I32),
+                in_=tab_scales[:, 4 * q : 4 * q + 4, :].bitcast(I32),
+            )
+        tab = [load_table(0)]
+        for q in range(4):
+            nc.sync.dma_start(
+                out=w4_scale_rows[32 * q : 32 * q + 4, :, :].bitcast(I32),
+                in_=w4_scales[:, 4 * q : 4 * q + 4, :].rearrange("g r n -> r g n").bitcast(I32),
+            )
         tab.append(load_table(1))
         room_sb = {}
-        room_sb[0, 0] = [load_room(0, 0, t, 1)[0] for t in range(4)]
-        room_sb[0, 1] = load_room(0, 1, 0, 4)
-        w1_raw[1, 0] = load_weight(w1, 0, 512)
-        w1_raw[1, 1] = load_weight(w1, 512, 512)
-        w3_raw = [load_weight(w3, 0, 0)]
-        room_sb[1, 0] = load_room(1, 0, 0, 4)
-        room_sb[1, 1] = load_room(1, 1, 0, 4)
-        w3_raw.append(load_weight(w3, 512, 0))
+        room_sb[0, 0] = load_room(0, 0, 0, 2) + load_room(0, 0, 2, 2)
+        w3_raw = {}
+        for what in LOADS:
+            if what[0] == "r":
+                room_sb[what[1], what[2]] = load_room(what[1], what[2], 0, 4)
+            elif what[0] == "w1":
+                w1_raw[1, what[1]] = load_weight(w1, 512 * what[1], 512)
+            else:
+                w3_raw[what[1]] = load_weight(w3, 512 * what[1], 0)
 
-        def round_weight(raw):
-            grouped = ring.tile([P, 4, P, 4], BF16, name="w_grouped", align_bytes=64)
-            src = raw[:].rearrange("p j (q t) -> p q j t", t=4)
+        def round_weight(raw, t0, engine="S"):
+            grouped = ring.tile([P, 2, P, 4], BF16, name="w_grouped", align_bytes=64, bufs=WB)
+            src = raw[:].rearrange("p j (q t) -> p q j t", t=4)[:, :, :, t0 : t0 + 2]
             dst = grouped[:].rearrange("p t q j -> p q j t")
-            for t0 in (0, 2):
-                nc.scalar.copy(out=dst[:, :, :, t0 : t0 + 2], in_=src[:, :, :, t0 : t0 + 2])
+            if engine == "S":
+                nc.scalar.copy(out=dst, in_=src)
+            else:
+                nc.vector.tensor_copy(out=dst, in_=src)
             return grouped
 
         def quantize(grouped_2d, width, name):
@@ -110,7 +120,7 @@ def tile_list_crate_pair_features_kernel(
             return codes, scales
 
         def quantize_weight(grouped, name):
-            return quantize(grouped[:].rearrange("p t q j -> p (t q j)"), BANK, name)
+            return quantize(grouped[:].rearrange("p t q j -> p (t q j)"), 2 * P, name)
 
         w4_codes = keep.tile([P, 2, 4, P, 2], U8, align_bytes=64)
         w4_sc = keep.tile([P, 2, 4, P], U8, align_bytes=64)
@@ -128,7 +138,8 @@ def tile_list_crate_pair_features_kernel(
 
         w1_q = {}
         for a in range(2):
-            w1_q[0, a] = quantize_weight(round_weight(w1_raw[0, a]), "w1_0_%d" % a)
+            for t0 in (0, 2):
+                w1_q[0, a, t0] = quantize_weight(round_weight(w1_raw[0, a], t0), "w1_0_%d_%d" % (a, t0))
         v_codes = {}
         for a in range(2):
             for half in range(2):
@@ -148,11 +159,12 @@ def tile_list_crate_pair_features_kernel(
             for t in range(4):
                 acc = psum.tile([P, BANK], F32, name="bank_%d" % (4 * half + t))
                 for a in range(2):
-                    codes, scales = w1_q[g, a]
+                    codes, scales = w1_q[g, a, t - t % 2]
+                    cols = slice(P * (t % 2), P * (t % 2) + P)
                     nc.tensor.matmul_mx(
                         out=acc[:],
-                        lhsT=codes[:, P * t : P * t + P].bitcast(FP8X4),
-                        lhsT_scale=scales[:, P * t : P * t + P],
+                        lhsT=codes[:, cols].bitcast(FP8X4),
+                        lhsT_scale=scales[:, cols],
                         rhs=v_codes[a, half][:].bitcast(FP8X4),
                         rhs_scale=v_scales[4 * a : P, BANK * half : BANK * half + BANK],
                         start=(a == 0),
@@ -166,60 +178,69 @@ def tile_list_crate_pair_features_kernel(
                 nc.scalar.activation(act[:, t, :], x[:], ACT.Silu)
             return act
 
-        def make_h(act, g, half):
-            grouped = ring.tile([P, BANK, 4], BF16, name="h_grouped", align_bytes=64)
-            nc.vector.tensor_tensor(
-                out=grouped[:].rearrange("p (c i) t -> p c t i", i=2),
-                in0=act[:].rearrange("p t (c i) -> p c t i", i=2),
-                in1=gain_pairs[:, g : g + 1, :, :].to_broadcast([P, BANK // 2, 4, 2]),
-                op=ALU.mult,
-            )
+        def make_h(act, g, half, how):
+            grouped = ring.tile([P, BANK, 4], BF16, name="h_grouped", align_bytes=64, bufs=HB)
+            c0 = 0
+            for cols, first, second in how:
+                c1 = c0 + cols
+                dst = grouped[:, c0:c1, :].rearrange("p (c i) t -> p c t i", i=2)
+                if first == "V":
+                    nc.vector.tensor_tensor(
+                        out=dst,
+                        in0=act[:, :, c0:c1].rearrange("p t (c i) -> p c t i", i=2),
+                        in1=gain_pairs[:, g : g + 1, :, :].to_broadcast([P, cols // 2, 4, 2]),
+                        op=ALU.mult,
+                    )
+                else:
+                    rounded = ring.tile([P, 4, cols], BF16, name="h_rounded")
+                    for t in range(4):
+                        if first == "S":
+                            nc.scalar.activation(
+                                rounded[:, t, :], act[:, t, c0:c1], ACT.Copy, scale=gain_sb[:, g, t : t + 1]
+                            )
+                        else:
+                            nc.gpsimd.tensor_scalar(
+                                rounded[:, t, :], act[:, t, c0:c1], gain_sb[:, g, t : t + 1], 0.0, ALU.mult, ALU.add
+                            )
+                    src = rounded[:].rearrange("p t (c i) -> p c t i", i=2)
+                    if second == "S":
+                        nc.scalar.copy(out=dst, in_=src)
+                    else:
+                        nc.vector.tensor_copy(out=dst, in_=src)
+                c0 = c1
             return quantize(grouped[:].rearrange("p j t -> p (j t)"), BANK, "h_%d_%d" % (g, half))
 
         h_q = {}
-        act00 = first_stage(0, 0)
-        act01 = first_stage(0, 1)
-        h_q[0, 0] = make_h(act00, 0, 0)
-        w1_q[1, 0] = quantize_weight(round_weight(w1_raw[1, 0]), "w1_1_0")
-        w1_q[1, 1] = quantize_weight(round_weight(w1_raw[1, 1]), "w1_1_1")
-        h_q[0, 1] = make_h(act01, 0, 1)
-        w3_grouped = round_weight(w3_raw[0])
-        act10 = first_stage(1, 0)
-        w3_q = [quantize_weight(w3_grouped, "w3_0")]
-        act11 = first_stage(1, 1)
-        w3_grouped = round_weight(w3_raw[1])
-        h_q[1, 0] = make_h(act10, 1, 0)
-        w3_q.append(quantize_weight(w3_grouped, "w3_1"))
-        h_q[1, 1] = make_h(act11, 1, 1)
-
         e = [keep.tile([P, S], F32, name="e_%d" % t) for t in range(4)]
-        for half in range(2):
-            for t in range(4):
-                dev = psum.tile([P, BANK], F32, name="bank_%d" % (2 * t))
-                low = psum.tile([P, BANK], F32, name="bank_%d" % (2 * t + 1))
-                for g in range(2):
-                    codes, scales = h_q[g, half]
-                    nc.tensor.matmul_mx(
-                        out=dev[:],
-                        lhsT=w3_q[g][0][:, P * t : P * t + P].bitcast(FP8X4),
-                        lhsT_scale=w3_q[g][1][:, P * t : P * t + P],
-                        rhs=codes[:].bitcast(FP8X4), rhs_scale=scales[:],
-                        start=(g == 0), stop=(g == 1),
-                    )
-                for g in range(2):
-                    codes, scales = h_q[g, half]
-                    nc.tensor.matmul_mx(
-                        out=low[:],
-                        lhsT=w4_codes[:, g, t].rearrange("p q b -> p (q b)").bitcast(FP4X4),
-                        lhsT_scale=w4_sc[:, g, t, :],
-                        rhs=codes[:].bitcast(FP8X4), rhs_scale=scales[:],
-                        start=(g == 0), stop=(g == 1),
-                    )
-                size = ring.tile([P, BANK], F32, name="size", bufs=4)
-                nc.scalar.activation(size[:], dev[:], ACT.Abs)
-                nc.vector.tensor_tensor(
-                    out=e[t][:, BANK * half : BANK * half + BANK], in0=low[:], in1=size[:], op=ALU.max
+        w3_q = {}
+
+        def second_stage(t, half, bank):
+            dev = psum.tile([P, BANK], F32, name="bank_%d" % bank)
+            low = psum.tile([P, BANK], F32, name="bank_%d" % (bank + 1))
+            cols = slice(P * (t % 2), P * (t % 2) + P)
+            for g in range(2):
+                codes, scales = h_q[g, half]
+                nc.tensor.matmul_mx(
+                    out=dev[:],
+                    lhsT=w3_q[g, t - t % 2][0][:, cols].bitcast(FP8X4),
+                    lhsT_scale=w3_q[g, t - t % 2][1][:, cols],
+                    rhs=codes[:].bitcast(FP8X4), rhs_scale=scales[:],
+                    start=(g == 0), stop=(g == 1),
                 )
+            for g in range(2):
+                codes, scales = h_q[g, half]
+                nc.tensor.matmul_mx(
+                    out=low[:],
+                    lhsT=w4_codes[:, g, t].rearrange("p q b -> p (q b)").bitcast(FP4X4),
+                    lhsT_scale=w4_sc[:, g, t, :],
+                    rhs=codes[:].bitcast(FP8X4), rhs_scale=scales[:],
+                    start=(g == 0), stop=(g == 1),
+                )
+            size = ring.tile([P, BANK], F32, name="size", bufs=4)
+            nc.scalar.activation(size[:], dev[:], ACT.Abs)
+            nc.vector.tensor_tensor(
+                out=e[t][:, BANK * half : BANK * half + BANK], in0=low[:], in1=size[:], op=ALU.max
+            )
 
         y_codes = keep.tile([P, M], I32, align_bytes=64)
         y_scales = keep.tile([P, M], U8, align_bytes=64)
@@ -244,12 +265,22 @@ def tile_list_crate_pair_features_kernel(
             )
             nc.sync.dma_start(out=out_words[:, m0 : m0 + width], in_=y_codes[:, m0 : m0 + width])
 
-        for t in range(3):
-            pair_up(t, 0, M)
-        pair_up(3, 0, 256)
-        pair_up(3, 256, 256)
-        planes(0, 256)
-        planes(256, 256)
+        acts = {}
+        for what in STEPS:
+            if what[0] == "A":
+                acts[what[1], what[2]] = first_stage(what[1], what[2])
+            elif what[0] == "C":
+                h_q[what[1], what[2]] = make_h(acts[what[1], what[2]], what[1], what[2], what[3])
+            elif what[0] == "w1":
+                w1_q[1, what[1], what[2]] = quantize_weight(round_weight(w1_raw[1, what[1]], what[2], what[3]), "w1_1_%d_%d" % (what[1], what[2]))
+            elif what[0] == "w3":
+                w3_q[what[1], what[2]] = quantize_weight(round_weight(w3_raw[what[1]], what[2], what[3]), "w3_%d_%d" % (what[1], what[2]))
+            elif what[0] == "E":
+                second_stage(what[1], what[2], what[3])
+            elif what[0] == "Y":
+                pair_up(what[1], what[2], what[3])
+            else:
+                planes(what[1], what[2])
         for q, queue in enumerate((nc.scalar, nc.sync, nc.scalar, nc.sync)):
             queue.dma_start(
                 out=out_2[0, 4 * q : 4 * q + 4, :].bitcast(I32),

@@ -17,14 +17,12 @@ ALU = mybir.AluOpType
 ACT = mybir.ActivationFunctionType
 
 P = 128
+PASS = 512
 BANK = 512
-HB = 1
-WB = 3
-V = [(512,"V","")]
-LOADS = [("r",0,1),("w1",0),("w1",1),("r",1,0),("r",1,1),("w3",0),("w3",1)]
-STEPS = [("A",0,0),("A",0,1),("w1",0,0,"S"),("w1",1,0,"S"),("w1",0,2,"S"),("w1",1,2,"S"),("C",0,0,V),("C",0,1,[(256,"V",""),(256,"S","S")]),("A",1,0),("A",1,1),("w3",0,0,"S"),("w3",1,0,"S"),("C",1,0,V),("C",1,1,V),
- ("E",0,0,0),("E",1,0,2),("E",0,1,4),("E",1,1,6),("w3",0,2,"S"),("w3",1,2,"S"),("Y",0,0,512),("E",2,0,0),("E",2,1,2),("Y",1,0,512),("E",3,0,4),("E",3,1,6),("Y",2,0,512),
- ("Y",3,0,256),("Y",3,256,256),("P",0,256),("P",256,256)]
+LIST_COLUMN = 16
+
+SCALAR_GAIN_COLUMNS = 256
+FIRST_PIECE, LAST_PIECE = 256, 128
 
 
 def tile_list_crate_pair_features_kernel(
@@ -39,201 +37,178 @@ def tile_list_crate_pair_features_kernel(
 
         tab_scale_rows = keep.tile([P, T], U8)
         w4_scale_rows = keep.tile([P, 2, N], U8)
-        nc.vector.memset(tab_scale_rows[:].bitcast(I32), 0)
+        v_scales = keep.tile([P, 2, S], U8, align_bytes=64)
         nc.vector.memset(w4_scale_rows[:].rearrange("p g n -> p (g n)").bitcast(I32), 0)
-
-        warm = keep.tile([P, 8], F32)
-        warm_out = keep.tile([P, 8], F32)
-        nc.vector.memset(warm[:], 0.0)
-        nc.scalar.activation(warm_out[:], warm[:], ACT.Silu)
+        nc.vector.memset(tab_scale_rows[32:64, :].bitcast(I32), 0)
+        nc.vector.memset(tab_scale_rows[64:P, :].bitcast(I32), 0)
+        nc.vector.memset(v_scales[:].rearrange("p a n -> p (a n)").bitcast(I32), 0)
 
         def load_weight(w, row0, col0):
-            raw = ring.tile([P, 4, BANK], F32, name="w_raw", bufs=4)
-            nc.sync.dma_start(
-                out=raw[:], in_=w[row0 : row0 + 512, col0 : col0 + BANK].rearrange("(p j) c -> p j c", j=4)
-            )
+            raw = ring.tile([P, 4, PASS], F32, name="w_raw", bufs=4)
+            rows = w[row0 : row0 + PASS, col0 : col0 + PASS]
+            nc.sync.dma_start(out=raw[:], in_=rows.rearrange("(p j) c -> p j c", j=4))
             return raw
-
-        def load_room(g, half, t0, nt):
-            raw = keep.tile([P, nt, BANK], F32, name="room_%d_%d_%d" % (g, half, t0))
-            rows = room[512 * g : 512 * g + 512, BANK * half : BANK * half + BANK].rearrange("(p t) j -> p t j", t=4)
-            nc.sync.dma_start(out=raw[:], in_=rows[:, t0 : t0 + nt, :])
-            return [raw[:, t, :] for t in range(nt)]
 
         def load_table(a):
             words = keep.tile([P, T], I32, name="tab_%d" % a)
             nc.sync.dma_start(out=words[:], in_=tab_words[a].rearrange("p n t -> p (n t)").bitcast(I32))
             return words
 
+        def load_room(g, slices, cols):
+            rows = room[PASS * g : PASS * g + PASS, :].rearrange("(p t) j -> p t j", t=4)
+            nc.sync.dma_start(out=room_sb[g][:, slices, cols], in_=rows[:, slices, cols])
+
         w1_raw = {}
         w1_raw[0, 0] = load_weight(w1, 0, 0)
-        idx = keep.tile([P, S // 16], U16)
+        idx = keep.tile([P, S // LIST_COLUMN], U16)
         nc.sync.dma_start(idx[:], offs)
-        w4_raw = keep.tile([P, 2, 2 * N], U8)
-        nc.sync.dma_start(out=w4_raw[:].bitcast(I32), in_=w4_words.rearrange("g p n -> p g n").bitcast(I32))
+        nc.sync.dma_start(
+            out=tab_scale_rows[0:32, :].bitcast(I32), in_=tab_scales.rearrange("a q n -> q a n").bitcast(I32)
+        )
+        w4_raw = []
+        for g in range(2):
+            w4_pass = keep.tile([P, 2 * N], U8, name="w4_raw_%d" % g)
+            nc.sync.dma_start(out=w4_pass[:].bitcast(I32), in_=w4_words[g].bitcast(I32))
+            w4_raw.append(w4_pass)
         sens_sb = keep.tile([P, 2, 4], F32)
         gain_sb = keep.tile([P, 2, 4], F32)
         nc.sync.dma_start(out=sens_sb[:], in_=sens.rearrange("(g p t) -> p g t", g=2, t=4))
         nc.sync.dma_start(out=gain_sb[:], in_=gain.rearrange("(g p t) -> p g t", g=2, t=4))
-        p1 = keep.tile([P, M // 16], U16)
-        p2 = keep.tile([P, M // 16], U16)
-        nc.sync.dma_start(p1[:], pos1)
-        nc.sync.dma_start(p2[:], pos2)
-        w1_raw[0, 1] = load_weight(w1, 512, 0)
-        for q in range(4):
+        w1_raw[0, 1] = load_weight(w1, PASS, 0)
+        for quad in range(4):
             nc.sync.dma_start(
-                out=tab_scale_rows[32 * q : 32 * q + 8, :].bitcast(I32),
-                in_=tab_scales[:, 4 * q : 4 * q + 4, :].bitcast(I32),
+                out=w4_scale_rows[32 * quad : 32 * quad + 4, :, :].bitcast(I32),
+                in_=w4_scales[:, 4 * quad : 4 * quad + 4, :].rearrange("g s n -> s g n").bitcast(I32),
             )
+        p1 = keep.tile([P, M // LIST_COLUMN], U16)
+        nc.sync.dma_start(p1[:], pos1)
+        p2 = keep.tile([P, M // LIST_COLUMN], U16)
+        nc.sync.dma_start(p2[:], pos2)
         tab = [load_table(0)]
-        for q in range(4):
+        picked_scale_rows = keep.tile([P, S], U8)
+        nc.vector.tensor_copy(picked_scale_rows[:], tab_scale_rows[:].indirect(idx[:]))
+        for quad in range(4):
             nc.sync.dma_start(
-                out=w4_scale_rows[32 * q : 32 * q + 4, :, :].bitcast(I32),
-                in_=w4_scales[:, 4 * q : 4 * q + 4, :].rearrange("g r n -> r g n").bitcast(I32),
+                out=v_scales[32 * quad : 32 * quad + 4, :, :].bitcast(I32),
+                in_=picked_scale_rows[8 * quad : 8 * quad + 8, :].bitcast(I32),
             )
         tab.append(load_table(1))
-        room_sb = {}
-        room_sb[0, 0] = load_room(0, 0, 0, 2) + load_room(0, 0, 2, 2)
-        w3_raw = {}
-        for what in LOADS:
-            if what[0] == "r":
-                room_sb[what[1], what[2]] = load_room(what[1], what[2], 0, 4)
-            elif what[0] == "w1":
-                w1_raw[1, what[1]] = load_weight(w1, 512 * what[1], 512)
-            else:
-                w3_raw[what[1]] = load_weight(w3, 512 * what[1], 0)
+        room_sb = [keep.tile([P, 4, S], F32, name="room_%d" % g) for g in range(2)]
+        load_room(0, slice(0, 2), slice(0, BANK))
+        load_room(0, slice(2, 4), slice(0, BANK))
+        load_room(0, slice(0, 4), slice(BANK, S))
+        w1_raw[1, 0] = load_weight(w1, 0, PASS)
+        w1_raw[1, 1] = load_weight(w1, PASS, PASS)
+        load_room(1, slice(0, 2), slice(0, S))
+        load_room(1, slice(2, 4), slice(0, S))
+        w3_raw = [load_weight(w3, 0, 0), load_weight(w3, PASS, 0)]
 
-        def round_weight(raw, t0, engine="S"):
-            grouped = ring.tile([P, 2, P, 4], BF16, name="w_grouped", align_bytes=64, bufs=WB)
-            src = raw[:].rearrange("p j (q t) -> p q j t", t=4)[:, :, :, t0 : t0 + 2]
-            dst = grouped[:].rearrange("p t q j -> p q j t")
-            if engine == "S":
-                nc.scalar.copy(out=dst, in_=src)
-            else:
-                nc.vector.tensor_copy(out=dst, in_=src)
-            return grouped
-
-        def quantize(grouped_2d, width, name):
+        def quantize(grouped, width, name):
             codes = keep.tile([P, width], I32, name=name + "_codes", align_bytes=64)
             scales = keep.tile([P, width], U8, name=name + "_scales", align_bytes=64)
-            nc.vector.quantize_mx(out=codes[:].bitcast(FP8X4), scales=scales[:], in_=grouped_2d)
+            nc.vector.quantize_mx(out=codes[:].bitcast(FP8X4), scales=scales[:], in_=grouped)
             return codes, scales
 
-        def quantize_weight(grouped, name):
+        def quantize_weight(raw, t0, name):
+            grouped = ring.tile([P, 2, P, 4], BF16, name="w_grouped", align_bytes=64, bufs=3)
+            nc.scalar.copy(
+                out=grouped[:].rearrange("p t q j -> p q j t"),
+                in_=raw[:].rearrange("p j (q t) -> p q j t", t=4)[:, :, :, t0 : t0 + 2],
+            )
             return quantize(grouped[:].rearrange("p t q j -> p (t q j)"), 2 * P, name)
+
+        def stationary(quantized, t):
+            codes, scales = quantized
+            cols = slice(P * (t % 2), P * (t % 2) + P)
+            return codes[:, cols].bitcast(FP8X4), scales[:, cols]
 
         w4_codes = keep.tile([P, 2, 4, P, 2], U8, align_bytes=64)
         w4_sc = keep.tile([P, 2, 4, P], U8, align_bytes=64)
         for g in range(2):
             nc.vector.tensor_copy(
                 out=w4_codes[:, g].rearrange("p t q b -> p q t b"),
-                in_=w4_raw[:, g, :].rearrange("p (q t b) -> p q t b", t=4, b=2),
+                in_=w4_raw[g][:].rearrange("p (q t b) -> p q t b", t=4, b=2),
             )
         gain_pairs = keep.tile([P, 2, 4, 2], F32)
         for i in range(2):
             nc.vector.tensor_copy(out=gain_pairs[:, :, :, i], in_=gain_sb[:])
 
-        v_scales = keep.tile([P, S], U8, align_bytes=64)
-        nc.vector.tensor_copy(v_scales[:], tab_scale_rows[:].indirect(idx[:]))
-
         w1_q = {}
         for a in range(2):
             for t0 in (0, 2):
-                w1_q[0, a, t0] = quantize_weight(round_weight(w1_raw[0, a], t0), "w1_0_%d_%d" % (a, t0))
+                w1_q[0, a, t0] = quantize_weight(w1_raw[0, a], t0, "w1_0_%d_%d" % (a, t0))
         v_codes = {}
         for a in range(2):
             for half in range(2):
                 picked = keep.tile([P, BANK], U32, name="v_%d_%d" % (a, half), align_bytes=64)
-                nc.vector.tensor_copy(
-                    picked[:], tab[a][:].bitcast(U32).indirect(idx[:, 32 * half : 32 * half + 32])
-                )
+                entries = slice(BANK // LIST_COLUMN * half, BANK // LIST_COLUMN * (half + 1))
+                nc.vector.tensor_copy(picked[:], tab[a][:].bitcast(U32).indirect(idx[:, entries]))
                 v_codes[a, half] = picked
-
         nc.vector.tensor_copy(
             out=w4_sc[:].rearrange("p g t q -> p g q t"),
             in_=w4_scale_rows[:].rearrange("p g (q t) -> p g q t", t=4),
         )
 
-        def first_stage(g, half):
-            act = ring.tile([P, 4, BANK], F32, name="act")
-            for t in range(4):
-                acc = psum.tile([P, BANK], F32, name="bank_%d" % (4 * half + t))
-                for a in range(2):
-                    codes, scales = w1_q[g, a, t - t % 2]
-                    cols = slice(P * (t % 2), P * (t % 2) + P)
-                    nc.tensor.matmul_mx(
-                        out=acc[:],
-                        lhsT=codes[:, cols].bitcast(FP8X4),
-                        lhsT_scale=scales[:, cols],
-                        rhs=v_codes[a, half][:].bitcast(FP8X4),
-                        rhs_scale=v_scales[4 * a : P, BANK * half : BANK * half + BANK],
-                        start=(a == 0),
-                        stop=(a == 1),
+        def first_stage(g):
+            for half in range(2):
+                cols = slice(BANK * half, BANK * half + BANK)
+                for t in range(4):
+                    acc = psum.tile([P, BANK], F32, name="bank_%d" % (4 * half + t))
+                    for a in range(2):
+                        codes, scales = stationary(w1_q[g, a, t - t % 2], t)
+                        nc.tensor.matmul_mx(
+                            out=acc[:], lhsT=codes, lhsT_scale=scales,
+                            rhs=v_codes[a, half][:].bitcast(FP8X4), rhs_scale=v_scales[:, a, cols],
+                            start=(a == 0), stop=(a == 1),
+                        )
+                    x = room_sb[g][:, t, cols]
+                    nc.vector.scalar_tensor_tensor(
+                        out=x, in0=acc[:], scalar=sens_sb[:, g, t : t + 1], in1=x, op0=ALU.mult, op1=ALU.add
                     )
-                x = ring.tile([P, BANK], F32, name="x", bufs=4)
-                nc.vector.scalar_tensor_tensor(
-                    out=x[:], in0=acc[:], scalar=sens_sb[:, g, t : t + 1], in1=room_sb[g, half][t],
-                    op0=ALU.mult, op1=ALU.add,
-                )
-                nc.scalar.activation(act[:, t, :], x[:], ACT.Silu)
-            return act
+                    nc.scalar.activation(x, x, ACT.Silu)
 
-        def make_h(act, g, half, how):
-            grouped = ring.tile([P, BANK, 4], BF16, name="h_grouped", align_bytes=64, bufs=HB)
-            c0 = 0
-            for cols, first, second in how:
-                c1 = c0 + cols
-                dst = grouped[:, c0:c1, :].rearrange("p (c i) t -> p c t i", i=2)
-                if first == "V":
-                    nc.vector.tensor_tensor(
-                        out=dst,
-                        in0=act[:, :, c0:c1].rearrange("p t (c i) -> p c t i", i=2),
-                        in1=gain_pairs[:, g : g + 1, :, :].to_broadcast([P, cols // 2, 4, 2]),
-                        op=ALU.mult,
+        def make_h(g, half, scalar_columns):
+            act = room_sb[g][:, :, BANK * half : BANK * half + BANK]
+            grouped = ring.tile([P, BANK, 4], BF16, name="h_grouped", align_bytes=64)
+            cut = BANK - scalar_columns
+            nc.vector.tensor_tensor(
+                out=grouped[:, 0:cut, :].rearrange("p (c i) t -> p c t i", i=2),
+                in0=act[:, :, 0:cut].rearrange("p t (c i) -> p c t i", i=2),
+                in1=gain_pairs[:, g : g + 1, :, :].to_broadcast([P, cut // 2, 4, 2]),
+                op=ALU.mult,
+            )
+            if scalar_columns:
+                rounded = ring.tile([P, 4, scalar_columns], BF16, name="h_rounded")
+                for t in range(4):
+                    nc.scalar.activation(
+                        rounded[:, t, :], act[:, t, cut:BANK], ACT.Copy, scale=gain_sb[:, g, t : t + 1]
                     )
-                else:
-                    rounded = ring.tile([P, 4, cols], BF16, name="h_rounded")
-                    for t in range(4):
-                        if first == "S":
-                            nc.scalar.activation(
-                                rounded[:, t, :], act[:, t, c0:c1], ACT.Copy, scale=gain_sb[:, g, t : t + 1]
-                            )
-                        else:
-                            nc.gpsimd.tensor_scalar(
-                                rounded[:, t, :], act[:, t, c0:c1], gain_sb[:, g, t : t + 1], 0.0, ALU.mult, ALU.add
-                            )
-                    src = rounded[:].rearrange("p t (c i) -> p c t i", i=2)
-                    if second == "S":
-                        nc.scalar.copy(out=dst, in_=src)
-                    else:
-                        nc.vector.tensor_copy(out=dst, in_=src)
-                c0 = c1
+                nc.scalar.copy(
+                    out=grouped[:, cut:BANK, :].rearrange("p (c i) t -> p c t i", i=2),
+                    in_=rounded[:].rearrange("p t (c i) -> p c t i", i=2),
+                )
             return quantize(grouped[:].rearrange("p j t -> p (j t)"), BANK, "h_%d_%d" % (g, half))
 
         h_q = {}
-        e = [keep.tile([P, S], F32, name="e_%d" % t) for t in range(4)]
         w3_q = {}
+        e = [keep.tile([P, S], F32, name="e_%d" % t) for t in range(4)]
 
         def second_stage(t, half, bank):
             dev = psum.tile([P, BANK], F32, name="bank_%d" % bank)
             low = psum.tile([P, BANK], F32, name="bank_%d" % (bank + 1))
-            cols = slice(P * (t % 2), P * (t % 2) + P)
             for g in range(2):
-                codes, scales = h_q[g, half]
+                codes, scales = stationary(w3_q[g, t - t % 2], t)
                 nc.tensor.matmul_mx(
-                    out=dev[:],
-                    lhsT=w3_q[g, t - t % 2][0][:, cols].bitcast(FP8X4),
-                    lhsT_scale=w3_q[g, t - t % 2][1][:, cols],
-                    rhs=codes[:].bitcast(FP8X4), rhs_scale=scales[:],
+                    out=dev[:], lhsT=codes, lhsT_scale=scales,
+                    rhs=h_q[g, half][0][:].bitcast(FP8X4), rhs_scale=h_q[g, half][1][:],
                     start=(g == 0), stop=(g == 1),
                 )
             for g in range(2):
-                codes, scales = h_q[g, half]
                 nc.tensor.matmul_mx(
                     out=low[:],
                     lhsT=w4_codes[:, g, t].rearrange("p q b -> p (q b)").bitcast(FP4X4),
                     lhsT_scale=w4_sc[:, g, t, :],
-                    rhs=codes[:].bitcast(FP8X4), rhs_scale=scales[:],
+                    rhs=h_q[g, half][0][:].bitcast(FP8X4), rhs_scale=h_q[g, half][1][:],
                     start=(g == 0), stop=(g == 1),
                 )
             size = ring.tile([P, BANK], F32, name="size", bufs=4)
@@ -245,44 +220,79 @@ def tile_list_crate_pair_features_kernel(
         y_codes = keep.tile([P, M], I32, align_bytes=64)
         y_scales = keep.tile([P, M], U8, align_bytes=64)
         y_grouped = keep.tile([P, M, 4], BF16, align_bytes=64)
+        y_rows = keep.tile([P, 4, M], F32)
         out_rows = out_0.rearrange("(p t) m -> p t m", t=4)
         out_words = out_1[0].rearrange("p m t -> p (m t)").bitcast(I32)
 
-        def pair_up(t, m0, width):
-            places = slice(m0 // 16, (m0 + width) // 16)
-            upper = ring.tile([P, width], F32, name="upper")
-            y = keep.tile([P, width], F32, name="y_%d_%d" % (t, m0))
-            nc.vector.tensor_copy(upper[:], e[t][:].indirect(p1[:, places]))
-            nc.vector.tensor_tensor(y[:], e[t][:].indirect(p2[:, places]), upper[:], ALU.add)
-            nc.scalar.copy(out=y_grouped[:, m0 : m0 + width, t], in_=y[:])
-            nc.sync.dma_start(out=out_rows[:, t, m0 : m0 + width], in_=y[:])
+        def pair_up(t, m0, m1):
+            entries = slice(m0 // LIST_COLUMN, m1 // LIST_COLUMN)
+            upper = ring.tile([P, m1 - m0], F32, name="upper")
+            nc.vector.tensor_copy(upper[:], e[t][:].indirect(p1[:, entries]))
+            nc.vector.tensor_tensor(y_rows[:, t, m0:m1], e[t][:].indirect(p2[:, entries]), upper[:], ALU.add)
 
-        def planes(m0, width):
-            nc.vector.quantize_mx(
-                out=y_codes[:, m0 : m0 + width].bitcast(FP8X4),
-                scales=y_scales[:, m0 : m0 + width],
-                in_=y_grouped[:, m0 : m0 + width, :].rearrange("p m t -> p (m t)"),
+        def round_y(copy, t0, m0, m1):
+            copy(
+                out=y_grouped[:, m0:m1, t0 : t0 + 2].rearrange("p (c i) t -> p c t i", i=2),
+                in_=y_rows[:, t0 : t0 + 2, m0:m1].rearrange("p t (c i) -> p c t i", i=2),
             )
-            nc.sync.dma_start(out=out_words[:, m0 : m0 + width], in_=y_codes[:, m0 : m0 + width])
 
-        acts = {}
-        for what in STEPS:
-            if what[0] == "A":
-                acts[what[1], what[2]] = first_stage(what[1], what[2])
-            elif what[0] == "C":
-                h_q[what[1], what[2]] = make_h(acts[what[1], what[2]], what[1], what[2], what[3])
-            elif what[0] == "w1":
-                w1_q[1, what[1], what[2]] = quantize_weight(round_weight(w1_raw[1, what[1]], what[2], what[3]), "w1_1_%d_%d" % (what[1], what[2]))
-            elif what[0] == "w3":
-                w3_q[what[1], what[2]] = quantize_weight(round_weight(w3_raw[what[1]], what[2], what[3]), "w3_%d_%d" % (what[1], what[2]))
-            elif what[0] == "E":
-                second_stage(what[1], what[2], what[3])
-            elif what[0] == "Y":
-                pair_up(what[1], what[2], what[3])
-            else:
-                planes(what[1], what[2])
-        for q, queue in enumerate((nc.scalar, nc.sync, nc.scalar, nc.sync)):
+        def store_y(t):
+            nc.sync.dma_start(out=out_rows[:, t, :], in_=y_rows[:, t, :])
+
+        def quantize_y(m0, m1):
+            nc.vector.quantize_mx(
+                out=y_codes[:, m0:m1].bitcast(FP8X4),
+                scales=y_scales[:, m0:m1],
+                in_=y_grouped[:, m0:m1, :].rearrange("p m t -> p (m t)"),
+            )
+
+        def store_words(m0, m1):
+            nc.sync.dma_start(out=out_words[:, m0:m1], in_=y_codes[:, m0:m1])
+
+        first_stage(0)
+        for t0 in (0, 2):
+            for a in range(2):
+                w1_q[1, a, t0] = quantize_weight(w1_raw[1, a], t0, "w1_1_%d_%d" % (a, t0))
+        h_q[0, 0] = make_h(0, 0, 0)
+        h_q[0, 1] = make_h(0, 1, SCALAR_GAIN_COLUMNS)
+        first_stage(1)
+        for g in range(2):
+            w3_q[g, 0] = quantize_weight(w3_raw[g], 0, "w3_%d_0" % g)
+        h_q[1, 0] = make_h(1, 0, 0)
+        h_q[1, 1] = make_h(1, 1, SCALAR_GAIN_COLUMNS)
+
+        for half in range(2):
+            for t in range(2):
+                second_stage(t, half, 4 * half + 2 * t)
+        for g in range(2):
+            w3_q[g, 2] = quantize_weight(w3_raw[g], 2, "w3_%d_2" % g)
+        pair_up(0, 0, M)
+        store_y(0)
+        for half in range(2):
+            second_stage(2, half, 2 * half)
+        pair_up(1, 0, M)
+        round_y(nc.scalar.copy, 0, 0, M)
+        store_y(1)
+        for half in range(2):
+            second_stage(3, half, 4 + 2 * half)
+        pair_up(2, 0, M)
+        store_y(2)
+
+        last = M - LAST_PIECE
+        pair_up(3, 0, FIRST_PIECE)
+        round_y(nc.scalar.copy, 2, 0, FIRST_PIECE)
+        pair_up(3, FIRST_PIECE, last)
+        round_y(nc.scalar.copy, 2, FIRST_PIECE, last)
+        quantize_y(0, FIRST_PIECE)
+        pair_up(3, last, M)
+        round_y(nc.vector.tensor_copy, 2, last, M)
+        store_y(3)
+        quantize_y(FIRST_PIECE, last)
+        store_words(0, last)
+        quantize_y(last, M)
+        store_words(last, M)
+        for quad, queue in enumerate((nc.scalar, nc.sync, nc.scalar, nc.sync)):
             queue.dma_start(
-                out=out_2[0, 4 * q : 4 * q + 4, :].bitcast(I32),
-                in_=y_scales[32 * q : 32 * q + 4, :].bitcast(I32),
+                out=out_2[0, 4 * quad : 4 * quad + 4, :].bitcast(I32),
+                in_=y_scales[32 * quad : 32 * quad + 4, :].bitcast(I32),
             )

@@ -129,9 +129,6 @@ def tile_list_crate_pair_features_kernel(
                 out=w4_codes[:, g].rearrange("p t q b -> p q t b"),
                 in_=w4_raw[g][:].rearrange("p (q t b) -> p q t b", t=4, b=2),
             )
-        gain_pairs = keep.tile([P, 2, 4, 2], F32)
-        for i in range(2):
-            nc.vector.tensor_copy(out=gain_pairs[:, :, :, i], in_=gain_sb[:])
 
         w1_q = {}
         for a in range(2):
@@ -171,10 +168,11 @@ def tile_list_crate_pair_features_kernel(
             act = room_sb[g][:, :, BANK * half : BANK * half + BANK]
             grouped = ring.tile([P, BANK, 4], BF16, name="h_grouped", align_bytes=64)
             cut = BANK - scalar_columns
+            gains = gain_sb[:, g : g + 1, :].rearrange("p c (t i) -> p c t i", i=1)
             nc.vector.tensor_tensor(
-                out=grouped[:, 0:cut, :].rearrange("p (c i) t -> p c t i", i=2),
-                in0=act[:, :, 0:cut].rearrange("p t (c i) -> p c t i", i=2),
-                in1=gain_pairs[:, g : g + 1, :, :].to_broadcast([P, cut // 2, 4, 2]),
+                out=grouped[:, 0:cut, :].rearrange("p (c i) t -> p c t i", i=4),
+                in0=act[:, :, 0:cut].rearrange("p t (c i) -> p c t i", i=4),
+                in1=gains.to_broadcast([P, cut // 4, 4, 4]),
                 op=ALU.mult,
             )
             if scalar_columns:
@@ -184,8 +182,8 @@ def tile_list_crate_pair_features_kernel(
                         rounded[:, t, :], act[:, t, cut:BANK], ACT.Copy, scale=gain_sb[:, g, t : t + 1]
                     )
                 nc.scalar.copy(
-                    out=grouped[:, cut:BANK, :].rearrange("p (c i) t -> p c t i", i=2),
-                    in_=rounded[:].rearrange("p t (c i) -> p c t i", i=2),
+                    out=grouped[:, cut:BANK, :].rearrange("p (c i) t -> p c t i", i=4),
+                    in_=rounded[:].rearrange("p t (c i) -> p c t i", i=4),
                 )
             return quantize(grouped[:].rearrange("p j t -> p (j t)"), BANK, "h_%d_%d" % (g, half))
 

from contextlib import ExitStack

import concourse.mybir as mybir

K, T, S, H, N, M = 1024, 4096, 1024, 1024, 512, 512
FLOPS = 2 * K * H * S + 2 * 2 * H * N * S

F32 = mybir.dt.float32
BF16 = mybir.dt.bfloat16
I32 = mybir.dt.int32
U32 = mybir.dt.uint32
U16 = mybir.dt.uint16
U8 = mybir.dt.uint8
FP8X4 = mybir.dt.float8_e4m3fn_x4
FP4X4 = mybir.dt.float4_e2m1fn_x4
ALU = mybir.AluOpType
ACT = mybir.ActivationFunctionType

P = 128
PASS = 512
BANK = 512
LIST_COLUMN = 16

SCALAR_GAIN_COLUMNS = 256
FIRST_PIECE, LAST_PIECE = 256, 128


def tile_list_crate_pair_features_kernel(
    tc, tab_words, tab_scales, offs, pos1, pos2, w1, sens, room, gain, w4_words, w4_scales, w3,
    out_0, out_1, out_2,
):
    nc = tc.nc
    with ExitStack() as ctx:
        keep = ctx.enter_context(tc.tile_pool(name="keep", bufs=1))
        ring = ctx.enter_context(tc.tile_pool(name="ring", bufs=2))
        psum = ctx.enter_context(tc.psum_pool(name="psum", bufs=1))

        tab_scale_rows = keep.tile([P, T], U8)
        w4_scale_rows = keep.tile([P, 2, N], U8)
        v_scales = keep.tile([P, 2, S], U8, align_bytes=64)
        nc.vector.memset(w4_scale_rows[:].rearrange("p g n -> p (g n)").bitcast(I32), 0)
        nc.vector.memset(tab_scale_rows[32:64, :].bitcast(I32), 0)
        nc.vector.memset(tab_scale_rows[64:P, :].bitcast(I32), 0)
        nc.vector.memset(v_scales[:].rearrange("p a n -> p (a n)").bitcast(I32), 0)

        def load_weight(w, row0, col0):
            raw = ring.tile([P, 4, PASS], F32, name="w_raw", bufs=4)
            rows = w[row0 : row0 + PASS, col0 : col0 + PASS]
            nc.sync.dma_start(out=raw[:], in_=rows.rearrange("(p j) c -> p j c", j=4))
            return raw

        def load_table(a):
            words = keep.tile([P, T], I32, name="tab_%d" % a)
            nc.sync.dma_start(out=words[:], in_=tab_words[a].rearrange("p n t -> p (n t)").bitcast(I32))
            return words

        def load_room(g, slices, cols):
            rows = room[PASS * g : PASS * g + PASS, :].rearrange("(p t) j -> p t j", t=4)
            nc.sync.dma_start(out=room_sb[g][:, slices, cols], in_=rows[:, slices, cols])

        w1_raw = {}
        w1_raw[0, 0] = load_weight(w1, 0, 0)
        idx = keep.tile([P, S // LIST_COLUMN], U16)
        nc.sync.dma_start(idx[:], offs)
        nc.sync.dma_start(
            out=tab_scale_rows[0:32, :].bitcast(I32), in_=tab_scales.rearrange("a q n -> q a n").bitcast(I32)
        )
        w4_raw = []
        for g in range(2):
            w4_pass = keep.tile([P, 2 * N], U8, name="w4_raw_%d" % g)
            nc.sync.dma_start(out=w4_pass[:].bitcast(I32), in_=w4_words[g].bitcast(I32))
            w4_raw.append(w4_pass)
        sens_sb = keep.tile([P, 2, 4], F32)
        gain_sb = keep.tile([P, 2, 4], F32)
        nc.sync.dma_start(out=sens_sb[:], in_=sens.rearrange("(g p t) -> p g t", g=2, t=4))
        nc.sync.dma_start(out=gain_sb[:], in_=gain.rearrange("(g p t) -> p g t", g=2, t=4))
        w1_raw[0, 1] = load_weight(w1, PASS, 0)
        for quad in range(4):
            nc.sync.dma_start(
                out=w4_scale_rows[32 * quad : 32 * quad + 4, :, :].bitcast(I32),
                in_=w4_scales[:, 4 * quad : 4 * quad + 4, :].rearrange("g s n -> s g n").bitcast(I32),
            )
        p1 = keep.tile([P, M // LIST_COLUMN], U16)
        nc.sync.dma_start(p1[:], pos1)
        p2 = keep.tile([P, M // LIST_COLUMN], U16)
        nc.sync.dma_start(p2[:], pos2)
        tab = [load_table(0)]
        picked_scale_rows = keep.tile([P, S], U8)
        nc.vector.tensor_copy(picked_scale_rows[:], tab_scale_rows[:].indirect(idx[:]))
        for quad in range(4):
            nc.sync.dma_start(
                out=v_scales[32 * quad : 32 * quad + 4, :, :].bitcast(I32),
                in_=picked_scale_rows[8 * quad : 8 * quad + 8, :].bitcast(I32),
            )
        tab.append(load_table(1))
        room_sb = [keep.tile([P, 4, S], F32, name="room_%d" % g) for g in range(2)]
        load_room(0, slice(0, 2), slice(0, BANK))
        load_room(0, slice(2, 4), slice(0, BANK))
        load_room(0, slice(0, 4), slice(BANK, S))
        w1_raw[1, 0] = load_weight(w1, 0, PASS)
        w1_raw[1, 1] = load_weight(w1, PASS, PASS)
        load_room(1, slice(0, 2), slice(0, S))
        load_room(1, slice(2, 4), slice(0, S))
        w3_raw = [load_weight(w3, 0, 0), load_weight(w3, PASS, 0)]

        def quantize(grouped, width, name):
            codes = keep.tile([P, width], I32, name=name + "_codes", align_bytes=64)
            scales = keep.tile([P, width], U8, name=name + "_scales", align_bytes=64)
            nc.vector.quantize_mx(out=codes[:].bitcast(FP8X4), scales=scales[:], in_=grouped)
            return codes, scales

        def quantize_weight(raw, t0, name):
            grouped = ring.tile([P, 2, P, 4], BF16, name="w_grouped", align_bytes=64, bufs=3)
            nc.scalar.copy(
                out=grouped[:].rearrange("p t q j -> p q j t"),
                in_=raw[:].rearrange("p j (q t) -> p q j t", t=4)[:, :, :, t0 : t0 + 2],
            )
            return quantize(grouped[:].rearrange("p t q j -> p (t q j)"), 2 * P, name)

        def stationary(quantized, t):
            codes, scales = quantized
            cols = slice(P * (t % 2), P * (t % 2) + P)
            return codes[:, cols].bitcast(FP8X4), scales[:, cols]

        w4_codes = keep.tile([P, 2, 4, P, 2], U8, align_bytes=64)
        w4_sc = keep.tile([P, 2, 4, P], U8, align_bytes=64)
        for g in range(2):
            nc.vector.tensor_copy(
                out=w4_codes[:, g].rearrange("p t q b -> p q t b"),
                in_=w4_raw[g][:].rearrange("p (q t b) -> p q t b", t=4, b=2),
            )

        w1_q = {}
        for a in range(2):
            for t0 in (0, 2):
                w1_q[0, a, t0] = quantize_weight(w1_raw[0, a], t0, "w1_0_%d_%d" % (a, t0))
        v_codes = {}
        for a in range(2):
            for half in range(2):
                picked = keep.tile([P, BANK], U32, name="v_%d_%d" % (a, half), align_bytes=64)
                entries = slice(BANK // LIST_COLUMN * half, BANK // LIST_COLUMN * (half + 1))
                nc.vector.tensor_copy(picked[:], tab[a][:].bitcast(U32).indirect(idx[:, entries]))
                v_codes[a, half] = picked
        nc.vector.tensor_copy(
            out=w4_sc[:].rearrange("p g t q -> p g q t"),
            in_=w4_scale_rows[:].rearrange("p g (q t) -> p g q t", t=4),
        )

        def first_stage(g):
            for half in range(2):
                cols = slice(BANK * half, BANK * half + BANK)
                for t in range(4):
                    acc = psum.tile([P, BANK], F32, name="bank_%d" % (4 * half + t))
                    for a in range(2):
                        codes, scales = stationary(w1_q[g, a, t - t % 2], t)
                        nc.tensor.matmul_mx(
                            out=acc[:], lhsT=codes, lhsT_scale=scales,
                            rhs=v_codes[a, half][:].bitcast(FP8X4), rhs_scale=v_scales[:, a, cols],
                            start=(a == 0), stop=(a == 1),
                        )
                    x = room_sb[g][:, t, cols]
                    nc.vector.scalar_tensor_tensor(
                        out=x, in0=acc[:], scalar=sens_sb[:, g, t : t + 1], in1=x, op0=ALU.mult, op1=ALU.add
                    )
                    nc.scalar.activation(x, x, ACT.Silu)

        def make_h(g, half, scalar_columns):
            act = room_sb[g][:, :, BANK * half : BANK * half + BANK]
            grouped = ring.tile([P, BANK, 4], BF16, name="h_grouped", align_bytes=64)
            cut = BANK - scalar_columns
            gains = gain_sb[:, g : g + 1, :].rearrange("p c (t i) -> p c t i", i=1)
            nc.vector.tensor_tensor(
                out=grouped[:, 0:cut, :].rearrange("p (c i) t -> p c t i", i=4),
                in0=act[:, :, 0:cut].rearrange("p t (c i) -> p c t i", i=4),
                in1=gains.to_broadcast([P, cut // 4, 4, 4]),
                op=ALU.mult,
            )
            if scalar_columns:
                rounded = ring.tile([P, 4, scalar_columns], BF16, name="h_rounded")
                for t in range(4):
                    nc.scalar.activation(
                        rounded[:, t, :], act[:, t, cut:BANK], ACT.Copy, scale=gain_sb[:, g, t : t + 1]
                    )
                nc.scalar.copy(
                    out=grouped[:, cut:BANK, :].rearrange("p (c i) t -> p c t i", i=4),
                    in_=rounded[:].rearrange("p t (c i) -> p c t i", i=4),
                )
            return quantize(grouped[:].rearrange("p j t -> p (j t)"), BANK, "h_%d_%d" % (g, half))

        h_q = {}
        w3_q = {}
        e = [keep.tile([P, S], F32, name="e_%d" % t) for t in range(4)]

        def second_stage(t, half, bank):
            dev = psum.tile([P, BANK], F32, name="bank_%d" % bank)
            low = psum.tile([P, BANK], F32, name="bank_%d" % (bank + 1))
            for g in range(2):
                codes, scales = stationary(w3_q[g, t - t % 2], t)
                nc.tensor.matmul_mx(
                    out=dev[:], lhsT=codes, lhsT_scale=scales,
                    rhs=h_q[g, half][0][:].bitcast(FP8X4), rhs_scale=h_q[g, half][1][:],
                    start=(g == 0), stop=(g == 1),
                )
            for g in range(2):
                nc.tensor.matmul_mx(
                    out=low[:],
                    lhsT=w4_codes[:, g, t].rearrange("p q b -> p (q b)").bitcast(FP4X4),
                    lhsT_scale=w4_sc[:, g, t, :],
                    rhs=h_q[g, half][0][:].bitcast(FP8X4), rhs_scale=h_q[g, half][1][:],
                    start=(g == 0), stop=(g == 1),
                )
            size = ring.tile([P, BANK], F32, name="size", bufs=4)
            nc.scalar.activation(size[:], dev[:], ACT.Abs)
            nc.vector.tensor_tensor(
                out=e[t][:, BANK * half : BANK * half + BANK], in0=low[:], in1=size[:], op=ALU.max
            )

        y_codes = keep.tile([P, M], I32, align_bytes=64)
        y_scales = keep.tile([P, M], U8, align_bytes=64)
        y_grouped = keep.tile([P, M, 4], BF16, align_bytes=64)
        y_rows = keep.tile([P, 4, M], F32)
        out_rows = out_0.rearrange("(p t) m -> p t m", t=4)
        out_words = out_1[0].rearrange("p m t -> p (m t)").bitcast(I32)

        def pair_up(t, m0, m1):
            entries = slice(m0 // LIST_COLUMN, m1 // LIST_COLUMN)
            upper = ring.tile([P, m1 - m0], F32, name="upper")
            nc.vector.tensor_copy(upper[:], e[t][:].indirect(p1[:, entries]))
            nc.vector.tensor_tensor(y_rows[:, t, m0:m1], e[t][:].indirect(p2[:, entries]), upper[:], ALU.add)

        def round_y(copy, t0, m0, m1):
            copy(
                out=y_grouped[:, m0:m1, t0 : t0 + 2].rearrange("p (c i) t -> p c t i", i=2),
                in_=y_rows[:, t0 : t0 + 2, m0:m1].rearrange("p t (c i) -> p c t i", i=2),
            )

        def store_y(t):
            nc.sync.dma_start(out=out_rows[:, t, :], in_=y_rows[:, t, :])

        def quantize_y(m0, m1):
            nc.vector.quantize_mx(
                out=y_codes[:, m0:m1].bitcast(FP8X4),
                scales=y_scales[:, m0:m1],
                in_=y_grouped[:, m0:m1, :].rearrange("p m t -> p (m t)"),
            )

        def store_words(m0, m1):
            nc.sync.dma_start(out=out_words[:, m0:m1], in_=y_codes[:, m0:m1])

        first_stage(0)
        for t0 in (0, 2):
            for a in range(2):
                w1_q[1, a, t0] = quantize_weight(w1_raw[1, a], t0, "w1_1_%d_%d" % (a, t0))
        h_q[0, 0] = make_h(0, 0, 0)
        h_q[0, 1] = make_h(0, 1, SCALAR_GAIN_COLUMNS)
        first_stage(1)
        for g in range(2):
            w3_q[g, 0] = quantize_weight(w3_raw[g], 0, "w3_%d_0" % g)
        h_q[1, 0] = make_h(1, 0, 0)
        h_q[1, 1] = make_h(1, 1, SCALAR_GAIN_COLUMNS)

        for half in range(2):
            for t in range(2):
                second_stage(t, half, 4 * half + 2 * t)
        for g in range(2):
            w3_q[g, 2] = quantize_weight(w3_raw[g], 2, "w3_%d_2" % g)
        pair_up(0, 0, M)
        store_y(0)
        for half in range(2):
            second_stage(2, half, 2 * half)
        pair_up(1, 0, M)
        round_y(nc.scalar.copy, 0, 0, M)
        store_y(1)
        for half in range(2):
            second_stage(3, half, 4 + 2 * half)
        pair_up(2, 0, M)
        store_y(2)

        last = M - LAST_PIECE
        pair_up(3, 0, FIRST_PIECE)
        round_y(nc.scalar.copy, 2, 0, FIRST_PIECE)
        pair_up(3, FIRST_PIECE, last)
        round_y(nc.scalar.copy, 2, FIRST_PIECE, last)
        quantize_y(0, FIRST_PIECE)
        pair_up(3, last, M)
        round_y(nc.vector.tensor_copy, 2, last, M)
        store_y(3)
        quantize_y(FIRST_PIECE, last)
        store_words(0, last)
        quantize_y(last, M)
        store_words(last, M)
        for quad, queue in enumerate((nc.scalar, nc.sync, nc.scalar, nc.sync)):
            queue.dma_start(
                out=out_2[0, 4 * quad : 4 * quad + 4, :].bitcast(I32),
                in_=y_scales[32 * quad : 32 * quad + 4, :].bitcast(I32),
            )
